import numpy as np, ml_dtypes
CORES = [176,177,178,179,180,181,182,183,304,305,306,307,308,309,310,311]
N = 16
def setup_inputs(rng):
    return {"x": rng.standard_normal((N, 128, 16), dtype=np.float32).astype(ml_dtypes.bfloat16)}
def reference(x):
    s = x.sum(axis=0, dtype=np.float64).astype(x.dtype)
    b = 16 // N
    return {"y": np.stack([s[:, r * b:(r + 1) * b] for r in range(N)])}

@@ -1,0 +1,49 @@
+import concourse.bass as bass
+
+SCRATCH = {
+    "xs": ("sbuf", [128, 16], "bfloat16"),
+    "land": ("sbuf", [128, 16], "bfloat16"),
+    "res": ("sbuf", [128, 1], "bfloat16"),
+}
+SEMAPHORES = ["ld", "a1", "a2", "sent", "st"]
+
+
+def rank_program(g, core, T, topo):
+    r = T.rank_of(core)
+    if r is None:
+        return
+    cores = T.cores
+    n = len(cores)
+    q = r ^ 1
+
+    g.dma_start(T.xs[:], T.x[:]).then_inc(T.sem.ld, 16)
+    g.wait_ge(T.sem.ld, 16)
+
+    off, on = 0, 8
+    transfers = []
+    for j in range(n):
+        f = j ^ 1
+        if f == r:
+            continue
+        dst = cores[f]
+        rid, pid = topo.addr(dst, core)
+        if topo.mask(core, dst) == 0xFFFF:
+            eng, on = on, on + 1
+        else:
+            eng, off = off, off + 1
+        transfers.append(bass.RemoteDMATransfer(
+            dst_ids=[bass.DstId(rid=rid, pnc=pid)], dma_engine_mask=1 << eng, remote_sem=T.sem.a1,
+            srcs=[T.xs[:, j:j + 1]], dsts=[T.land[:, r:r + 1]], alu_op=0))
+    g.remote_dma_fused(transfers, local_sem=T.sem.sent)
+
+    g.wait_ge(T.sem.a1, n - 1)
+    srcs = [T.xs[:, q:q + 1] if k == r else T.land[:, k:k + 1] for k in range(n)]
+    rid, pid = topo.addr(cores[q], core)
+    g.remote_dma_fused([bass.RemoteDMATransfer(
+        dst_ids=[bass.DstId(rid=rid, pnc=pid)], dma_engine_mask=0xFFFF, remote_sem=T.sem.a2,
+        srcs=srcs, dsts=[T.res[:]], alu_op=1)], local_sem=T.sem.sent)
+
+    g.wait_ge(T.sem.a2, 16)
+    g.dma_start(T.y[:], T.res[:]).then_inc(T.sem.st, 16)
+    g.wait_ge(T.sem.sent, (n - 1) + 16)
+    g.wait_ge(T.sem.st, 16)

@@ -1,11 +1,26 @@
 import concourse.bass as bass
 
+N = 16
+NCH = 4
+W = 16 // NCH
+
 SCRATCH = {
-    "xs": ("sbuf", [128, 16], "bfloat16"),
-    "land": ("sbuf", [128, 16], "bfloat16"),
-    "res": ("sbuf", [128, 1], "bfloat16"),
+    "xs": ("dram", [NCH, 128, W], "bfloat16"),
+    "land": ("dram", [N, 128, W], "bfloat16"),
+    "s": ("dram", [NCH, 128, W], "bfloat16"),
 }
 SEMAPHORES = ["ld", "a1", "a2", "sent", "st"]
+
+
+def folders(Q):
+    return [2 * Q, 2 * Q + 1, 8 + 2 * Q, 8 + 2 * Q + 1]
+
+
+def server(Q, d):
+    base = (d // 8) * 8 + 2 * Q
+    if d // 2 == base // 2:
+        return d ^ 1
+    return base + d % 2
 
 
 def rank_program(g, core, T, topo):
@@ -13,37 +28,37 @@ def rank_program(g, core, T, topo):
     if r is None:
         return
     cores = T.cores
-    n = len(cores)
-    q = r ^ 1
+    P = (r % 8) // 2
+
+    def ids(ds):
+        out = []
+        for d in ds:
+            rid, pid = topo.addr(cores[d], core)
+            out.append(bass.DstId(rid=rid, pnc=pid))
+        return out
 
     g.dma_start(T.xs[:], T.x[:]).then_inc(T.sem.ld, 16)
     g.wait_ge(T.sem.ld, 16)
 
-    off, on = 0, 8
     transfers = []
-    for j in range(n):
-        f = j ^ 1
-        if f == r:
-            continue
-        dst = cores[f]
-        rid, pid = topo.addr(dst, core)
-        if topo.mask(core, dst) == 0xFFFF:
-            eng, on = on, on + 1
-        else:
-            eng, off = off, off + 1
-        transfers.append(bass.RemoteDMATransfer(
-            dst_ids=[bass.DstId(rid=rid, pnc=pid)], dma_engine_mask=1 << eng, remote_sem=T.sem.a1,
-            srcs=[T.xs[:, j:j + 1]], dsts=[T.land[:, r:r + 1]], alu_op=0))
+    for Q in range(NCH):
+        far = [d for d in folders(Q) if d // 8 != r // 8]
+        near = [d for d in folders(Q) if d // 8 == r // 8 and d != r]
+        for ds, lo in ((far, 0), (near, 8)):
+            transfers.append(bass.RemoteDMATransfer(
+                dst_ids=ids(ds), dma_engine_mask=0b11 << (lo + 2 * Q), remote_sem=T.sem.a1,
+                srcs=[T.xs[Q]], dsts=[T.land[r] for d in ds], alu_op=0))
     g.remote_dma_fused(transfers, local_sem=T.sem.sent)
 
-    g.wait_ge(T.sem.a1, n - 1)
-    srcs = [T.xs[:, q:q + 1] if k == r else T.land[:, k:k + 1] for k in range(n)]
-    rid, pid = topo.addr(cores[q], core)
+    g.wait_ge(T.sem.a1, 2 * (N - 1))
+    ds = [d for d in range(N) if d != r and server(P, d) == r]
     g.remote_dma_fused([bass.RemoteDMATransfer(
-        dst_ids=[bass.DstId(rid=rid, pnc=pid)], dma_engine_mask=0xFFFF, remote_sem=T.sem.a2,
-        srcs=srcs, dsts=[T.res[:]], alu_op=1)], local_sem=T.sem.sent)
+        dst_ids=ids(ds), dma_engine_mask=0xFFFF, remote_sem=T.sem.a2,
+        srcs=[T.xs[P] if k == r else T.land[k] for k in range(N)], dsts=[T.s[P] for d in ds], alu_op=1)],
+        local_sem=T.sem.sent)
 
-    g.wait_ge(T.sem.a2, 16)
-    g.dma_start(T.y[:], T.res[:]).then_inc(T.sem.st, 16)
-    g.wait_ge(T.sem.sent, (n - 1) + 16)
+    g.wait_ge(T.sem.a2, 16 * NCH)
+    g.dma_start(T.y[:], T.s[:, (r // W)::(16 // W), (r % W):(r % W) + 1],
+                allow_slow_non_contiguous=True).then_inc(T.sem.st, 16)
+    g.wait_ge(T.sem.sent, 2 * 2 * NCH + 16)
     g.wait_ge(T.sem.st, 16)

@@ -1,19 +1,17 @@
 import concourse.bass as bass
 
 N = 16
+HC = 8
 NCH = 4
-W = 16 // NCH
+W = HC // NCH
 
 SCRATCH = {
-    "xs": ("dram", [NCH, 128, W], "bfloat16"),
+    "xf": ("dram", [NCH, 128, W], "bfloat16"),
+    "xn": ("dram", [NCH, 128, W], "bfloat16"),
     "land": ("dram", [N, 128, W], "bfloat16"),
     "s": ("dram", [NCH, 128, W], "bfloat16"),
 }
-SEMAPHORES = ["ld", "a1", "a2", "sent", "st"]
-
-
-def folders(Q):
-    return [2 * Q, 2 * Q + 1, 8 + 2 * Q, 8 + 2 * Q + 1]
+SEMAPHORES = ["ldf", "ldn", "a1", "a2", "sent", "st"]
 
 
 def server(Q, d):
@@ -28,6 +26,8 @@ def rank_program(g, core, T, topo):
     if r is None:
         return
     cores = T.cores
+    home = (r // 8) * 8
+    away = 8 - home
     P = (r % 8) // 2
 
     def ids(ds):
@@ -37,28 +37,32 @@ def rank_program(g, core, T, topo):
             out.append(bass.DstId(rid=rid, pnc=pid))
         return out
 
-    g.dma_start(T.xs[:], T.x[:]).then_inc(T.sem.ld, 16)
-    g.wait_ge(T.sem.ld, 16)
-
-    transfers = []
-    for Q in range(NCH):
-        far = [d for d in folders(Q) if d // 8 != r // 8]
-        near = [d for d in folders(Q) if d // 8 == r // 8 and d != r]
-        for ds, lo in ((far, 0), (near, 8)):
+    def send(buf, base, lo):
+        transfers = []
+        for Q in range(NCH):
+            ds = [d for d in (base + 2 * Q, base + 2 * Q + 1) if d != r]
             transfers.append(bass.RemoteDMATransfer(
                 dst_ids=ids(ds), dma_engine_mask=0b11 << (lo + 2 * Q), remote_sem=T.sem.a1,
-                srcs=[T.xs[Q]], dsts=[T.land[r] for d in ds], alu_op=0))
-    g.remote_dma_fused(transfers, local_sem=T.sem.sent)
+                srcs=[buf[Q]], dsts=[T.land[r] for d in ds], alu_op=0))
+        g.remote_dma_fused(transfers, local_sem=T.sem.sent)
+
+    g.dma_start(T.xf[:], T.x[:, away:away + HC]).then_inc(T.sem.ldf, 16)
+    g.dma_start(T.xn[:], T.x[:, home:home + HC]).then_inc(T.sem.ldn, 16)
+    g.wait_ge(T.sem.ldf, 16)
+    send(T.xf, away, 0)
+    g.wait_ge(T.sem.ldn, 16)
+    send(T.xn, home, 8)
 
     g.wait_ge(T.sem.a1, 2 * (N - 1))
     ds = [d for d in range(N) if d != r and server(P, d) == r]
     g.remote_dma_fused([bass.RemoteDMATransfer(
         dst_ids=ids(ds), dma_engine_mask=0xFFFF, remote_sem=T.sem.a2,
-        srcs=[T.xs[P] if k == r else T.land[k] for k in range(N)], dsts=[T.s[P] for d in ds], alu_op=1)],
+        srcs=[T.xn[P] if k == r else T.land[k] for k in range(N)], dsts=[T.s[P] for d in ds], alu_op=1)],
         local_sem=T.sem.sent)
 
     g.wait_ge(T.sem.a2, 16 * NCH)
-    g.dma_start(T.y[:], T.s[:, (r // W)::(16 // W), (r % W):(r % W) + 1],
+    c = r % 8
+    g.dma_start(T.y[:], T.s[:, (c // W)::(HC // W), (c % W):(c % W) + 1],
                 allow_slow_non_contiguous=True).then_inc(T.sem.st, 16)
     g.wait_ge(T.sem.sent, 2 * 2 * NCH + 16)
     g.wait_ge(T.sem.st, 16)

import concourse.bass as bass

N = 16
HC = 8
NCH = 4
W = HC // NCH

SCRATCH = {
    "xf": ("dram", [NCH, 128, W], "bfloat16"),
    "xn": ("dram", [NCH, 128, W], "bfloat16"),
    "land": ("dram", [N, 128, W], "bfloat16"),
    "s": ("dram", [NCH, 128, W], "bfloat16"),
}
SEMAPHORES = ["ldf", "ldn", "a1", "a2", "sent", "st"]


def server(Q, d):
    base = (d // 8) * 8 + 2 * Q
    if d // 2 == base // 2:
        return d ^ 1
    return base + d % 2


def rank_program(g, core, T, topo):
    r = T.rank_of(core)
    if r is None:
        return
    cores = T.cores
    home = (r // 8) * 8
    away = 8 - home
    P = (r % 8) // 2

    def ids(ds):
        out = []
        for d in ds:
            rid, pid = topo.addr(cores[d], core)
            out.append(bass.DstId(rid=rid, pnc=pid))
        return out

    def send(buf, base, lo):
        transfers = []
        for Q in range(NCH):
            ds = [d for d in (base + 2 * Q, base + 2 * Q + 1) if d != r]
            transfers.append(bass.RemoteDMATransfer(
                dst_ids=ids(ds), dma_engine_mask=0b11 << (lo + 2 * Q), remote_sem=T.sem.a1,
                srcs=[buf[Q]], dsts=[T.land[r] for d in ds], alu_op=0))
        g.remote_dma_fused(transfers, local_sem=T.sem.sent)

    g.dma_start(T.xf[:], T.x[:, away:away + HC]).then_inc(T.sem.ldf, 16)
    g.dma_start(T.xn[:], T.x[:, home:home + HC]).then_inc(T.sem.ldn, 16)
    g.wait_ge(T.sem.ldf, 16)
    send(T.xf, away, 0)
    g.wait_ge(T.sem.ldn, 16)
    send(T.xn, home, 8)

    g.wait_ge(T.sem.a1, 2 * (N - 1))
    ds = [d for d in range(N) if d != r and server(P, d) == r]
    g.remote_dma_fused([bass.RemoteDMATransfer(
        dst_ids=ids(ds), dma_engine_mask=0xFFFF, remote_sem=T.sem.a2,
        srcs=[T.xn[P] if k == r else T.land[k] for k in range(N)], dsts=[T.s[P] for d in ds], alu_op=1)],
        local_sem=T.sem.sent)

    g.wait_ge(T.sem.a2, 16 * NCH)
    c = r % 8
    g.dma_start(T.y[:], T.s[:, (c // W)::(HC // W), (c % W):(c % W) + 1],
                allow_slow_non_contiguous=True).then_inc(T.sem.st, 16)
    g.wait_ge(T.sem.sent, 2 * 2 * NCH + 16)
    g.wait_ge(T.sem.st, 16)
